import numpy as np
import ml_dtypes


def mxq(x, axis, fmt="e4m3"):
    dtype, down = {"e4m3": (ml_dtypes.float8_e4m3fn, 7), "e5m2": (ml_dtypes.float8_e5m2, 14)}[fmt]
    v = np.moveaxis(np.asarray(x, np.float32).astype(ml_dtypes.bfloat16).astype(np.float64), axis, -1)
    blocks = v.reshape(v.shape[:-1] + (-1, 32))
    amax = np.abs(blocks).max(-1, keepdims=True)
    byte = np.maximum(np.where(amax > 0, np.frexp(amax)[1] - 1 + 127, 0) - down, 1)
    scale = np.exp2(byte - 127.0)
    codes = (blocks / scale).astype(np.float32).astype(dtype).astype(np.float64)
    return np.moveaxis((codes * scale).reshape(v.shape), -1, axis)


WIDE = False


def mx_kscale(k):
    if not WIDE:
        return np.ones(k)
    levels = np.array([10, -10, 5, -5, 0])
    if k % 512:
        return np.exp2(np.random.permutation(np.resize(levels, k // 32))).repeat(32)
    a = np.empty((k // 512, 16))
    for p in range(k // 512):
        a[p, :8] = np.random.permutation(np.resize(levels, 8))
        for g in range(8):
            far = levels[np.abs(levels - a[p, g]) >= 10]
            a[p, g + 8] = far[np.random.randint(len(far))]
    return np.exp2(a.ravel()).repeat(32)


BF16 = ml_dtypes.bfloat16


def bf(x):
    return np.asarray(x, np.float32).astype(BF16)


def f64(x):
    return np.asarray(x).astype(np.float64)


T, D, C, F, S = 1024, 1024, 512, 1024, 512
EPS = 1e-5


def sigmoid(z):
    return 1.0 / (1.0 + np.exp(-z))


def elu(z):
    return np.maximum(z, 0.0) + np.exp(np.minimum(z, 0.0)) - 1.0


def layer_norm(a, gain, shift):
    d = a - a.mean(axis=1, keepdims=True)
    return d / np.sqrt((d * d).mean(axis=1, keepdims=True) + EPS) * gain + shift


def setup_inputs():
    rn = np.random.standard_normal
    s, e = mx_kscale(D), mx_kscale(C)
    t = mx_kscale(F)
    u = mx_kscale(T)
    return {"x": bf(rn((T, D)) * s),
            "k": bf(rn((T, C)) * e),
            "w_x": bf(rn((D, F)) / np.sqrt(D) / s[:, None]),
            "w_k": bf(rn((C, F)) / np.sqrt(C) / e[:, None]),
            "b_h": bf(0.3 * rn(F)),
            "v": bf((1.0 + 0.1 * rn(F)) * t),
            "r": bf(np.random.uniform(0.5, 1.5, T) * u),
            "w_f": bf(rn((F, 2 * D)) / np.sqrt(F) / t[:, None]),
            "b_f": bf(0.3 * rn(2 * D)),
            "q": bf((1.0 + 0.1 * rn(T)) / u),
            "skip": bf((1.0 + 0.1 * rn(D)) / s),
            "g_y": bf(1.0 + 0.1 * rn(D)),
            "c_y": bf(0.2 * rn(D)),
            "a_t": bf(rn((2 * S, T)) / np.sqrt(T) / u),
            "b_t": bf(0.3 * rn(2 * S)),
            "n": bf((1.0 + 0.1 * rn(F)) / t),
            "p": bf(rn((S, F))),
            "g_z": bf(1.0 + 0.1 * rn(F)),
            "c_z": bf(0.2 * rn(F))}


def reference(x, k, w_x, w_k, b_h, v, r, w_f, b_f, q, skip, g_y, c_y, a_t, b_t, n, p, g_z, c_z):
    zx = mxq(f64(x), 1, "e4m3") @ mxq(f64(w_x), 0, "e4m3")
    zk = mxq(f64(k), 1, "e4m3") @ mxq(f64(w_k), 0, "e4m3")
    h = elu(zx + zk + f64(b_h)) * f64(v) * f64(r)[:, None]
    f = mxq(h, 1, "e4m3") @ mxq(f64(w_f), 0, "e4m3")
    f = f * f64(q)[:, None] + f64(b_f)
    y = layer_norm(f64(x) * f64(skip) + sigmoid(f[:, :D]) * f[:, D:], f64(g_y), f64(c_y))
    m = mxq(f64(a_t), 1, "e4m3") @ mxq(h, 0, "e4m3")
    m = m * f64(n) + f64(b_t)[:, None]
    z = layer_norm(f64(p) + sigmoid(m[:S]) * m[S:], f64(g_z), f64(c_z))
    return y, z

from contextlib import ExitStack

import concourse.mybir as mybir
from concourse.masks import make_identity

T, D, C, F, S = 1024, 1024, 512, 1024, 512
EPS = 1e-5
FLOPS = 2 * (T * (D + C) * F + T * F * 2 * D + 2 * S * T * F)

F32 = mybir.dt.float32
BF16 = mybir.dt.bfloat16
U32 = mybir.dt.uint32
U8 = mybir.dt.uint8
FP8X4 = mybir.dt.float8_e4m3fn_x4
ALU = mybir.AluOpType
ACT = mybir.ActivationFunctionType

P = 128
PACK = 4
KP = P * PACK
NB = 512


def tile_temporal_fusion_grn_f6_kernel(
    tc, x, k, w_x, w_k, b_h, v, r, w_f, b_f, q, skip, g_y, c_y, a_t, b_t, n, p, g_z, c_z, y_out, z_out
):
    nc = tc.nc
    with ExitStack() as ctx:
        keep = ctx.enter_context(tc.tile_pool(name="keep", bufs=1))
        ring = ctx.enter_context(tc.tile_pool(name="ring", bufs=1))
        psum = ctx.enter_context(tc.psum_pool(name="psum", bufs=8))
        ctx.enter_context(tc.manual_schedule(engines={mybir.EngineType.PE, mybir.EngineType.SP}))

        raw = {}
        staged = {}
        quant = {}
        state = {}

        def blk(i, width=KP):
            return slice(i * width, (i + 1) * width)

        def load_weight(key, w, g, nb):
            t = state["loads"].tile([P, PACK, KP], BF16, name="raw", tag="raw", bufs=12)
            nc.sync.dma_start(out=t[:], in_=w[blk(g), blk(nb)].rearrange("(p j) n -> p j n", j=PACK))
            raw[key] = t

        def load_rows(key, src, half):
            t = state["loads"].tile([P, 2, 2 * KP], BF16, name="raw", tag="raw", bufs=12)
            nc.sync.dma_start(out=t[:], in_=src[blk(half, 2 * P), :].rearrange("(i p) d -> p i d", p=P))
            raw[key, half] = t

        def load_k(c):
            t = state["loads"].tile([P, PACK, KP], BF16, name="raw", tag="raw", bufs=12)
            nc.sync.dma_start(out=t[:], in_=k[blk(c), :].rearrange("(i p) d -> p i d", p=P))
            raw["k", c] = t

        def load_broadcast(name, vec, width):
            t = keep.tile([P, width], BF16, name=name)
            nc.sync.dma_start(out=t[:], in_=vec.partition_broadcast(P))
            state[name] = t

        def load_channel_columns(name, vec, groups, queue):
            t = keep.tile([P, groups, PACK], BF16, name=name)
            queue.dma_start(out=t[:], in_=vec.rearrange("(g p j) -> p g j", g=groups, j=PACK))
            state[name] = t

        def stage_tile():
            return ring.tile([P, KP, PACK], BF16, name="staged", tag="staged", bufs=4, align_bytes=64)

        def copy_on(engine, out, in_):
            if engine == "V":
                nc.vector.tensor_copy(out=out, in_=in_)
            else:
                nc.scalar.copy(out=out, in_=in_)

        def interleave(key, src, engine, part=0, parts=1):
            if part == 0:
                staged[key] = stage_tile()
            cols = blk(part, KP // parts)
            copy_on(
                engine,
                staged[key][:, cols, :].rearrange("p (c i) j -> p c j i", i=4),
                src[:, :, cols].rearrange("p j (c i) -> p c j i", i=4),
            )

        def interleave_permuted(key, engine):
            staged[key] = stage_tile()
            copy_on(
                engine,
                staged[key][:].rearrange("p (t m) j -> p t m j", t=PACK),
                raw[key][:].rearrange("p j (m t) -> p t m j", t=PACK),
            )

        def turn(key, sources, half, engine, dst=None):
            if half == 0:
                staged[key] = stage_tile() if dst is None else dst
            bank = psum.tile([P, 2, 2, P], F32, name="bank", tag="bank")
            for i in range(2):
                words = sources[2 * half + i].bitcast(F32)
                for u in range(2):
                    nc.tensor.transpose(bank[:, i, u, :], words[:, u : 2 * P : 2], ident32[:])
            out = staged[key][:, blk(half, 2 * P), :].rearrange("p c j -> p (c j)").bitcast(F32)
            copy_on(engine, out.rearrange("p (i c u) -> p i c u", i=2, u=2), bank[:].rearrange("p i u c -> p i c u"))

        def row_sources(name, c, g):
            return [raw[name, 2 * c + i // 2][:, i % 2, blk(g)] for i in range(4)]

        def turn_x(c, g, half, engine="S"):
            turn(("x", c, g), row_sources("x", c, g), half, engine, dst=x_t[:, g, blk(c), :])

        def turn_k(c, half, engine="S"):
            turn(("k", c), [raw["k", c][:, i, :] for i in range(4)], half, engine)

        def turn_a(rc, c, half, engine="S"):
            turn(("a", rc, c), row_sources("a", rc, c), half, engine)

        def turn_h(g, c, half, engine="S"):
            turn(("ht", g, c), [h_t[:, g, j, blk(c)] for j in range(4)], half, engine)

        def quantize(key):
            codes = ring.tile([P, KP], U32, name="codes", tag="codes", bufs=24, align_bytes=64)
            scales = ring.tile([P, KP], U8, name="scales", tag="scales", bufs=24, align_bytes=64)
            nc.vector.quantize_mx(
                out=codes[:].bitcast(FP8X4), scales=scales[:], in_=staged[key].rearrange("p c j -> p (c j)")
            )
            quant[key] = (codes, scales)

        def mx_group(bank, pairs, cols):
            for i, (stat, mov) in enumerate(pairs):
                nc.tensor.matmul_mx(
                    out=bank,
                    lhsT=quant[stat][0][:, cols].bitcast(FP8X4),
                    lhsT_scale=quant[stat][1][:, cols],
                    rhs=quant[mov][0][:].bitcast(FP8X4),
                    rhs_scale=quant[mov][1][:],
                    start=(i == 0),
                    stop=(i == len(pairs) - 1),
                )

        def work_tile():
            return ring.tile([P, 2, NB], F32, name="work", tag="work", bufs=7)

        def new_bank():
            return psum.tile([P, NB], F32, name="bank", tag="bank")

        def hidden_front(c, g, j):
            bank = new_bank()
            pairs = [(("wk", g), ("k", c)), (("wx", 0, g), ("x", c, 0)), (("wx", 1, g), ("x", c, 1))]
            mx_group(bank[:], pairs, blk(j, P))
            w = work_tile()
            nc.scalar.activation(out=w[:, 0, :], in_=bank[:], func=ACT.Exp, bias=state["bh_col"][:, g, j : j + 1])
            nc.scalar.activation(out=w[:, 1, :], in_=bank[:], func=ACT.Relu, bias=state["bh_col"][:, g, j : j + 1])
            state["h", c, g, j] = w

        def hidden_elu(c, g, j):
            w = state["h", c, g, j]
            nc.vector.scalar_tensor_tensor(
                out=w[:, 0, :], in0=w[:, 0, :], scalar=-1.0, in1=w[:, 1, :], op0=ALU.add, op1=ALU.min
            )

        def hidden_scale(c, g, j):
            w = state["h", c, g, j]
            nc.vector.scalar_tensor_tensor(
                out=h_t[:, g, j, blk(c)],
                in0=w[:, 0, :],
                scalar=state["v_col"][:, g, j : j + 1],
                in1=state["r_b"][:, blk(c)],
                op0=ALU.mult,
                op1=ALU.mult,
            )

        NZ = S // P

        def token_tile(tile):
            return tile if tile < 2 * NZ else tile - 2 * NZ

        def natural(bank):
            return bank.rearrange("s (j m) -> s m j", j=PACK)

        def split(ap):
            return ap.rearrange("s (m j) -> s m j", j=PACK)

        def linear(tile, half):
            w = work_tile()
            state["lin", tile, half] = w
            for b in range(2):
                bank = new_bank()
                if tile < NZ:
                    mx_group(bank[:], [(("a", half, c), ("ht", b, c)) for c in range(2)], blk(tile, P))
                    nc.vector.tensor_tensor(
                        out=split(w[:, b, :]), in0=natural(bank[:]), in1=split(state["n_b"][:, blk(b)]), op=ALU.mult
                    )
                else:
                    i = token_tile(tile)
                    nb = 2 * half + b
                    mx_group(bank[:], [(("hf", i // 4, g), ("wf", g, nb)) for g in range(2)], blk(i % 4, P))
                    nc.vector.scalar_tensor_tensor(
                        out=w[:, b, :],
                        in0=bank[:],
                        scalar=cols[:, i : i + 1],
                        in1=state["bf_b"][:, blk(nb)],
                        op0=ALU.mult,
                        op1=ALU.add,
                    )

        def flat(w):
            return w[:].rearrange("s b n -> s (b n)")

        def gate(tile):
            w = flat(state["lin", tile, 0])
            if tile < NZ:
                nc.scalar.activation(out=w, in_=w, func=ACT.Sigmoid, bias=cols[:, 8 + tile : 9 + tile])
            else:
                nc.scalar.activation(out=w, in_=w, func=ACT.Sigmoid)

        def product(tile):
            sig = flat(state["lin", tile, 0])
            val = flat(state["lin", tile, 1])
            if tile < NZ:
                nc.vector.scalar_tensor_tensor(
                    out=val, in0=val, scalar=cols[:, 12 + tile : 13 + tile], in1=sig, op0=ALU.add, op1=ALU.mult
                )
            else:
                nc.vector.tensor_tensor(out=val, in0=val, in1=sig, op=ALU.mult)

        def residual(tile):
            w = state["lin", tile, 1]
            if tile < NZ:
                nc.vector.scalar_tensor_tensor(
                    out=flat(w), in0=flat(w), scalar=1.0, in1=p_sb[:, tile, :], op0=ALU.mult, op1=ALU.add,
                    accum_out=sums[:, tile, 0:1],
                )
            else:
                i = token_tile(tile)
                for g in range(2):
                    bank = new_bank()
                    for j in range(PACK):
                        nc.tensor.matmul(
                            bank[:, blk(j, P)], lhsT=x_t[:, g, blk(i, P), j], rhs=diag[:, g, j, :], start=True, stop=True
                        )
                    nc.vector.scalar_tensor_tensor(
                        out=split(w[:, g, :]), in0=natural(bank[:]), scalar=1.0, in1=split(w[:, g, :]),
                        op0=ALU.mult, op1=ALU.add, accum_out=sums[:, tile, g : g + 1],
                    )

        def scaled(g, i):
            w = state["late"].tile([P, 2, NB], F32, name="lin", tag="lin", bufs=6)
            state["scaled", g, i] = w
            for half in range(2):
                bank = new_bank()
                mx_group(bank[:], [(("hf", 0, e), ("wf", e, 2 * half + g)) for e in range(2)], blk(i, P))
                nc.scalar.activation(
                    out=w[:, half, :].rearrange("s (j m) -> s j m", j=PACK),
                    in_=bank[:].rearrange("s (m j) -> s j m", j=PACK),
                    func=ACT.Copy,
                    scale=cols[:, i : i + 1],
                )

        def turned_gate(g, j):
            banks = [new_bank(), new_bank()]
            for half in range(2):
                for i in range(4):
                    nc.tensor.transpose(banks[half][:, blk(i, P)], state["scaled", g, i][:, half, blk(j, P)], ident32[:])
            w = state["late"].tile([P, NB], F32, name="gated", tag="gated", bufs=8)
            nc.scalar.activation(out=w[:], in_=banks[0][:], func=ACT.Sigmoid, bias=state["bf_col"][:, g, j : j + 1])
            state["gated", g, j] = (w, banks[1])

        def turned_product(g, j):
            w, bank = state["gated", g, j]
            nc.vector.scalar_tensor_tensor(
                out=w[:], in0=bank[:], scalar=state["bf_col"][:, 2 + g, j : j + 1], in1=w[:], op0=ALU.add, op1=ALU.mult
            )

        def turned_residual(tile):
            i = token_tile(tile)
            w = work_tile()
            state["lin", tile, 1] = w
            banks = [new_bank(), new_bank()]
            for g in range(2):
                for j in range(PACK):
                    nc.tensor.matmul(
                        banks[g][:, blk(j, P)], lhsT=state["gated", g, j][0][:, blk(i, P)], rhs=ident32[:],
                        start=(j == 0), stop=False, is_transpose=True,
                    )
            for g in range(2):
                for j in range(PACK):
                    nc.tensor.matmul(
                        banks[g][:, blk(j, P)], lhsT=x_t[:, g, blk(i, P), j], rhs=diag[:, g, j, :],
                        start=False, stop=(j == PACK - 1),
                    )
            for g in range(2):
                nc.scalar.activation(
                    out=split(w[:, g, :]), in_=natural(banks[g][:]), func=ACT.Copy, accum_out=s_sums[:, tile, g : g + 1]
                )

        def statistics(tile):
            w = flat(state["lin", tile, 1])
            parts = 1 if tile < NZ else 2
            nc.scalar.activation(
                out=s_stats[:, tile, 2 : 2 + parts], in_=(sums if tile < 2 * NZ else s_sums)[:, tile, 0:parts], func=ACT.Copy, scale=-1.0 / D,
                accum_out=s_stats[:, tile, 0:1],
            )
            nc.scalar.activation(
                out=junk[:], in_=w, func=ACT.Square, bias=s_stats[:, tile, 0:1], accum_out=s_stats[:, tile, 1:2]
            )
            nc.gpsimd.tensor_scalar(
                out=g_stats[:, tile, 0:1], in0=s_stats[:, tile, 1:2], scalar1=1.0 / D, scalar2=EPS,
                op0=ALU.mult, op1=ALU.add,
            )
            nc.gpsimd.tensor_tensor(
                out=g_stats[:, tile, 1:2], in0=g_stats[:, tile, 0:1], in1=minus_half[:, 0:1], op=ALU.pow
            )

        def centre(tile):
            w = flat(state["lin", tile, 1])
            gain = state["gz_b" if tile < NZ else "gy_b"]
            nc.vector.scalar_tensor_tensor(
                out=w, in0=w, scalar=s_stats[:, tile, 0:1], in1=gain[:], op0=ALU.add, op1=ALU.mult
            )

        def finish(tile):
            w = flat(state["lin", tile, 1])
            shift = state["cz_b" if tile < NZ else "cy_b"]
            nc.vector.scalar_tensor_tensor(
                out=w, in0=w, scalar=g_stats[:, tile, 1:2], in1=shift[:], op0=ALU.mult, op1=ALU.add
            )
            dst = z_out[blk(tile, P), :] if tile < NZ else y_out[blk(token_tile(tile), P), :]
            nc.sync.dma_start(out=dst, in_=w)

        ident32 = keep.tile([P, P], F32, name="ident32")
        ident16 = keep.tile([P, P], BF16, name="ident16")
        rows = keep.tile([P, P], BF16, name="rows")
        cols = keep.tile([P, 16], F32, name="cols")
        diag = keep.tile([P, 2, PACK, P], BF16, name="diag")
        x_t = keep.tile([P, 2, T, PACK], BF16, name="x_t", align_bytes=64)
        h_t = keep.tile([P, 2, PACK, T], BF16, name="h_t")
        p_sb = keep.tile([P, NZ, F], BF16, name="p_sb")
        junk = keep.tile([P, D], BF16, name="junk")
        sums = keep.tile([P, 12, 8], F32, name="sums")
        s_sums = keep.tile([P, 12, 8], F32, name="s_sums")
        s_stats = keep.tile([P, 12, 8], F32, name="s_stats")
        g_stats = keep.tile([P, 12, 8], F32, name="g_stats")
        minus_half = keep.tile([P, 8], F32, name="minus_half")

        def wf_part(g, nb, part, engine="S"):
            interleave(("wf", g, nb), raw["wf", g, nb], engine, part, 2)

        def hf_part(c, g, part, engine="S"):
            interleave(("hf", c, g), h_t[:, g, :, blk(c)], engine, part, 2)

        def first_stage():
            make_identity(nc, ident32[:])
            load_k(0)
            load_weight(("wk", 0), w_k, 0, 0)
            load_rows("x", x, 0)
            load_rows("x", x, 1)
            load_weight(("wx", 0, 0), w_x, 0, 0)
            load_weight(("wx", 1, 0), w_x, 1, 0)
            load_channel_columns("bh_col", b_h, 2, nc.scalar)
            load_channel_columns("v_col", v, 2, nc.scalar)
            load_channel_columns("skip_col", skip, 2, nc.scalar)
            nc.gpsimd.memset(rows[:], 0.0)
            make_identity(nc, ident16[:])
            nc.gpsimd.memset(minus_half[:], -0.5)
            load_broadcast("r_b", r, T)
            load_k(1)
            load_rows("x", x, 2)
            load_rows("x", x, 3)
            load_weight(("wk", 1), w_k, 0, 1)
            load_weight(("wx", 0, 1), w_x, 0, 1)
            load_weight(("wx", 1, 1), w_x, 1, 1)
            nc.sync.dma_start(out=rows[0:8, :], in_=q.rearrange("(i p) -> i p", p=P))
            nc.sync.dma_start(out=rows[8:16, :], in_=b_t.rearrange("(i p) -> i p", p=P))
            load_channel_columns("bf_col", b_f, 4, nc.sync)
            for g in range(2):
                for j in range(PACK):
                    nc.gpsimd.tensor_scalar(
                        out=diag[:, g, j, :], in0=ident16[:], scalar1=state["skip_col"][:, g, j : j + 1], scalar2=0.0,
                        op0=ALU.mult, op1=ALU.add,
                    )

            def vector_columns():
                bank = psum.tile([P, P], BF16, name="bank", tag="bank")
                nc.tensor.transpose(bank[:], rows[:], ident16[:])
                nc.scalar.copy(out=cols[:], in_=bank[:, 0:16])

            turn_k(0, 0)
            turn_k(0, 1)
            interleave_permuted(("wk", 0), "V")
            turn_x(0, 0, 0)
            turn_x(0, 0, 1)
            quantize(("k", 0))
            turn_x(0, 1, 0)
            turn_x(0, 1, 1)
            quantize(("wk", 0))
            interleave_permuted(("wx", 0, 0), "V")
            quantize(("x", 0, 0))
            interleave_permuted(("wx", 1, 0), "S")
            quantize(("wx", 0, 0))
            quantize(("x", 0, 1))
            for half in range(4):
                load_rows("a", a_t, half)
            load_broadcast("n_b", n, F)
            quantize(("wx", 1, 0))

            def late_loads():
                for half in range(2):
                    nc.sync.dma_start(
                        out=p_sb[:, blk(half, 2), :], in_=p[blk(half, 2 * P), :].rearrange("(i s) f -> s i f", s=P)
                    )
                load_broadcast("gz_b", g_z, F)
                load_broadcast("cz_b", c_z, F)

            def load_wf(nb):
                for g in range(2):
                    load_weight(("wf", g, nb), w_f, g, nb)

            extra = {
                0: [lambda: turn_k(1, 0), lambda: turn_k(1, 1), lambda: interleave_permuted(("wk", 1), "V")],
                1: [lambda: turn_x(1, 0, 0), lambda: turn_x(1, 0, 1), lambda: quantize(("k", 1))],
                2: [lambda: turn_x(1, 1, 0), lambda: turn_x(1, 1, 1), lambda: quantize(("x", 1, 0))],
                3: [lambda: quantize(("wk", 1)), lambda: quantize(("x", 1, 1))],
                4: [lambda: interleave_permuted(("wx", 0, 1), "V"), late_loads],
                5: [lambda: quantize(("wx", 0, 1)), lambda: turn_h(0, 0, 0), lambda: load_wf(0)],
                6: [lambda: interleave_permuted(("wx", 1, 1), "V"), lambda: turn_h(0, 0, 1), lambda: load_wf(1)],
                7: [lambda: quantize(("wx", 1, 1)), lambda: quantize(("ht", 0, 0)), lambda: turn_a(0, 0, 0), lambda: turn_a(0, 0, 1)],
                8: [lambda: turn_a(0, 1, 0), lambda: turn_a(0, 1, 1), lambda: quantize(("a", 0, 0))],
                9: [lambda: turn_h(0, 1, 0), lambda: quantize(("a", 0, 1))],
                10: [lambda: turn_h(0, 1, 1), lambda: turn_a(1, 0, 0)],
                11: [lambda: turn_a(1, 0, 1), lambda: quantize(("ht", 0, 1))],
                12: [lambda: turn_a(1, 1, 0), lambda: quantize(("a", 1, 0)), lambda: load_wf(2), lambda: load_wf(3)],
                13: [lambda: turn_a(1, 1, 1), lambda: turn_h(1, 0, 0)],
                14: [lambda: turn_h(1, 0, 1), lambda: quantize(("a", 1, 1))],
                15: [vector_columns, lambda: quantize(("ht", 1, 0)), lambda: load_broadcast("bf_b", b_f, 2 * D),
                     lambda: load_broadcast("gy_b", g_y, D), lambda: load_broadcast("cy_b", c_y, D)],
            }
            tiles = [(c, g, j) for g in range(2) for c in range(2) for j in range(PACK)]
            for s in range(len(tiles) + 2):
                if s < len(tiles):
                    hidden_front(*tiles[s])
                if 1 <= s <= len(tiles):
                    hidden_elu(*tiles[s - 1])
                for job in extra.get(s, []):
                    job()
                if s >= 2:
                    hidden_scale(*tiles[s - 2])

            turn_h(1, 1, 0)
            wf_part(0, 0, 0, "V")
            turn_h(1, 1, 1)
            wf_part(0, 0, 1, "V")
            wf_part(1, 0, 0, "V")
            quantize(("ht", 1, 1))
            wf_part(1, 0, 1, "V")
            quantize(("wf", 0, 0))

        def prepare(key, part, engine="S"):
            (wf_part if key[0] == "wf" else hf_part)(key[1], key[2], part, engine)

        def prep(key, engine="S"):
            return [lambda: prepare(key, 0, engine), lambda: prepare(key, 1, engine)]

        def qz(*keys):
            return [lambda key=key: quantize(key) for key in keys]

        def sc(g, *tiles_):
            return [lambda i=i: scaled(g, i) for i in tiles_]

        def tg(g, *js):
            return [lambda j=j: turned_gate(g, j) for j in js]

        def tp(g, *js):
            return [lambda j=j: turned_product(g, j) for j in js]

        def call(f, tile):
            return [lambda: f(tile)]

        plan = {
            0: [prep(("wf", 0, 2)), qz(("wf", 1, 0)) + prep(("wf", 1, 2)), qz(("wf", 0, 2)) + prep(("wf", 0, 1)), qz(("wf", 1, 2))],
            1: [prep(("wf", 1, 1)), qz(("wf", 0, 1)), prep(("wf", 0, 3)), qz(("wf", 1, 1))],
            2: [prep(("wf", 1, 3)), qz(("wf", 0, 3)), prep(("hf", 0, 0)), qz(("wf", 1, 3)) + prep(("hf", 1, 0), "V")],
            3: [prep(("hf", 0, 1)), qz(("hf", 0, 0), ("hf", 1, 0)), prep(("hf", 1, 1)) + qz(("hf", 0, 1)), qz(("hf", 1, 1))],
            4: [sc(0, 0), sc(0, 1), sc(0, 2), sc(0, 3)],
            5: [tg(0, 0), tp(0, 0) + tg(0, 1) + sc(1, 0), tp(0, 1) + tg(0, 2), tp(0, 2) + tg(0, 3) + sc(1, 1)],
            6: [tp(0, 3) + sc(1, 2), sc(1, 3), tg(1, 0), tp(1, 0) + tg(1, 1)],
            7: [tp(1, 1) + tg(1, 2), tp(1, 2) + tg(1, 3), tp(1, 3), []],
        }
        n_rows = 2 * NZ

        def row_round(t):
            slots = plan.get(t, [[], [], [], []])
            if t >= 2:
                statistics(t - 2)
            if t < n_rows:
                linear(t, 0)
            for job in slots[0]:
                job()
            if t < n_rows:
                gate(t)
            if t == n_rows:
                turned_residual(t)
            if 1 <= t:
                product(t - 1)
            for job in slots[1]:
                job()
            if t >= 2:
                centre(t - 2)
            for job in slots[2]:
                job()
            if t < n_rows:
                linear(t, 1)
            if 1 <= t:
                residual(t - 1)
            for job in slots[3]:
                job()
            if t >= 2:
                finish(t - 2)

        with tc.tile_pool(name="loads", bufs=1) as loads:
            state["loads"] = loads
            first_stage()
            for t in range(NZ):
                row_round(t)
        state["late"] = ctx.enter_context(tc.tile_pool(name="late", bufs=1))
        for t in range(NZ, n_rows + 1):
            row_round(t)
        order = [8, 7, 9, 10, 11]
        for s in range(len(order) + 1):
            if s < len(order):
                statistics(order[s])
            if s + 2 < len(order):
                turned_residual(order[s + 2])
            if s < len(order):
                centre(order[s])
            if s >= 1:
                finish(order[s - 1])
